import numpy as np
import ml_dtypes


def mxq(x, axis, fmt="e4m3"):
    dtype, down = {"e4m3": (ml_dtypes.float8_e4m3fn, 7), "e5m2": (ml_dtypes.float8_e5m2, 14)}[fmt]
    v = np.moveaxis(np.asarray(x, np.float32).astype(ml_dtypes.bfloat16).astype(np.float64), axis, -1)
    blocks = v.reshape(v.shape[:-1] + (-1, 32))
    amax = np.abs(blocks).max(-1, keepdims=True)
    byte = np.maximum(np.where(amax > 0, np.frexp(amax)[1] - 1 + 127, 0) - down, 1)
    scale = np.exp2(byte - 127.0)
    codes = (blocks / scale).astype(np.float32).astype(dtype).astype(np.float64)
    return np.moveaxis((codes * scale).reshape(v.shape), -1, axis)


WIDE = False


def mx_kscale(k):
    if not WIDE:
        return np.ones(k)
    levels = np.array([10, -10, 5, -5, 0])
    if k % 512:
        return np.exp2(np.random.permutation(np.resize(levels, k // 32))).repeat(32)
    a = np.empty((k // 512, 16))
    for p in range(k // 512):
        a[p, :8] = np.random.permutation(np.resize(levels, 8))
        for g in range(8):
            far = levels[np.abs(levels - a[p, g]) >= 10]
            a[p, g + 8] = far[np.random.randint(len(far))]
    return np.exp2(a.ravel()).repeat(32)


def f64(x):
    return np.asarray(x).astype(np.float64)


def striped(idx):
    return np.tile(idx.reshape(-1, 16).T, (8, 1)).astype(np.uint16)


def unstriped(offs):
    return offs[:16].T.reshape(-1).astype(np.int64)


def pack_weight(w):
    k, n = w.shape
    w = f64(np.asarray(w, np.float32).astype(ml_dtypes.bfloat16)).reshape(k // 32, 32, n)
    amax = np.abs(w).max(1)
    byte = np.clip(np.where(amax > 0, np.frexp(amax)[1] - 1 + 127 - 7, 1), 1, 254)
    scaled = (w * np.exp2(127.0 - byte)[:, None, :]).reshape(k, n).astype(np.float32)
    words = np.ascontiguousarray(scaled.reshape(k // 512, 128, 4, n).transpose(0, 1, 3, 2)).astype(ml_dtypes.float8_e4m3fn).view(np.uint8)
    return words, np.ascontiguousarray(byte.astype(np.uint8).reshape(k // 512, 16, n))


def unpack_weight(words, scales):
    g, p, n, _ = words.shape
    vals = np.ascontiguousarray(words).view(ml_dtypes.float8_e4m3fn).astype(np.float64) * np.repeat(np.exp2(scales.astype(np.float64) - 127.0), 8, axis=1)[..., None]
    return vals.transpose(0, 1, 3, 2).reshape(g * 512, n)


K, T, S, H, V, Z, W = 512, 2048, 512, 512, 256, 512, 2048
P = 2 ** 7


def setup_inputs():
    n = np.random.standard_normal
    s = mx_kscale(K)[:, None]
    packed_xT = pack_weight(n((K, T)) * s)
    packed_eT = pack_weight(n((K, W)) * s)
    return {
        "x_words": packed_xT[0],
        "x_scales": packed_xT[1],
        "w1": (n((K, H)) / np.sqrt(K) / s).astype(np.float32),
        "e_words": packed_eT[0],
        "e_scales": packed_eT[1],
        "exq": (n((H, V))).astype(np.float32),
        "unit": (np.random.uniform(0.6, 1.4, (K, 1)) / np.sqrt(K) / s).astype(np.float32),
        "wgt": (np.tile(np.random.uniform(0.2, 1.4, W), (P, 1))).astype(np.float32),
        "offs": striped(np.random.permutation(T)[:S]),
        "bm1": striped(np.random.permutation(S)),
        "bm2": striped(np.random.permutation(S)),
        "ps": striped(np.random.permutation(S)[:V]),
        "prt": striped(np.random.permutation(W)[:Z]),
        "anc": striped(np.random.permutation(Z)),
    }


def reference(x_words, x_scales, w1, e_words, e_scales, exq, unit, wgt, offs, bm1, bm2, ps, prt, anc):
    xq = unpack_weight(x_words, x_scales)[:, unstriped(offs)]
    y = mxq(f64(w1), 0, "e4m3").T @ xq
    y1 = y[:, unstriped(bm1)]
    y2 = y[:, unstriped(bm2)]
    rng_ = np.minimum(y, y1) + np.maximum(y, y2)
    inn = rng_[:, unstriped(ps)] - f64(exq)
    hid = f64(unit) * inn
    e_prt = unpack_weight(e_words, e_scales)[:, unstriped(prt)]
    sc = mxq(hid, 0, "e4m3").T @ e_prt
    ll = -2.0 * ((np.tanh(sc)) ** 2)
    pw_ = np.exp(ll) * (f64(wgt)[:1][:, unstriped(prt)])
    tot = pw_.mean(axis=1, keepdims=True)
    nw = pw_ / (tot + 0.1)
    return nw + 0.5 * nw[:, unstriped(anc)]

@@ -1,0 +1,257 @@
+from contextlib import ExitStack
+
+import concourse.mybir as mybir
+
+K, T, S, H, V, Z, W = 512, 2048, 512, 512, 256, 512, 2048
+FLOPS = 2 * K * H * S + 2 * H * V * Z
+
+F32 = mybir.dt.float32
+BF16 = mybir.dt.bfloat16
+I32 = mybir.dt.int32
+U32 = mybir.dt.uint32
+U16 = mybir.dt.uint16
+U8 = mybir.dt.uint8
+FP8X4 = mybir.dt.float8_e4m3fn_x4
+ALU = mybir.AluOpType
+ACT = mybir.ActivationFunctionType
+
+P = 128
+PACK = 4
+PER_COL = 16
+
+
+def entries(offsets, first, count):
+    return offsets[:, first // PER_COL : (first + count) // PER_COL]
+
+
+def tile_picked_ymaprel_res_p_kernel(
+    tc, x_words, x_scales, w1, e_words, e_scales, exq, unit, wgt, offs, bm1, bm2, ps, prt, anc, out
+):
+    nc = tc.nc
+    with ExitStack() as ctx:
+        sb = ctx.enter_context(tc.tile_pool(name="sb", bufs=1))
+        psum = ctx.enter_context(tc.psum_pool(name="psum", bufs=1))
+
+        def load_list(name, src):
+            tile = sb.tile(list(src.shape), U16, name=name)
+            nc.sync.dma_start(tile[:], src)
+            return tile
+
+        def load_words(name, src):
+            tile = sb.tile([P, src.shape[2]], U32, name=name)
+            nc.sync.dma_start(tile[:].bitcast(I32), src[0].rearrange("p n t -> p (n t)").bitcast(I32))
+            return tile
+
+        def load_scales(name, src, queue):
+            tile = sb.tile([P, src.shape[2]], U8, name=name)
+            nc.vector.memset(tile[:].bitcast(I32), 0)
+            for q in range(4):
+                queue.dma_start(tile[32 * q : 32 * q + 4, :].bitcast(I32), src[0, 4 * q : 4 * q + 4, :].bitcast(I32))
+            return tile
+
+        def gathered(name, table, offsets, dtype):
+            tile = sb.tile([P, offsets.shape[1] * PER_COL], dtype, name=name, align_bytes=64)
+            nc.vector.tensor_copy(tile[:], table[:].indirect(offsets[:]))
+            return tile
+
+        offs_sb = load_list("offs_sb", offs)
+        w_raw = sb.tile([P, PACK, H], F32, name="w_raw")
+        nc.sync.dma_start(w_raw[:], w1.rearrange("(p j) c -> p j c", j=PACK))
+        x_scale_table = load_scales("x_scale_table", x_scales, nc.sync)
+        x_word_table = load_words("x_word_table", x_words)
+        bm1_sb = load_list("bm1_sb", bm1)
+        bm2_sb = load_list("bm2_sb", bm2)
+        prt_sb = load_list("prt_sb", prt)
+        e_scale_table = load_scales("e_scale_table", e_scales, nc.sync)
+        exq_sb = sb.tile([P, PACK, V], F32, name="exq_sb")
+        nc.sync.dma_start(exq_sb[:], exq.rearrange("(p t) v -> p t v", t=PACK))
+        ps_sb = load_list("ps_sb", ps)
+        unit_sb = sb.tile([P, PACK], F32, name="unit_sb")
+        nc.sync.dma_start(unit_sb[:], unit.rearrange("(p t) o -> p (t o)", t=PACK))
+        wgt_sb = sb.tile([P, W], F32, name="wgt_sb")
+        nc.sync.dma_start(wgt_sb[:], wgt)
+        e_word_table = load_words("e_word_table", e_words)
+        anc_sb = load_list("anc_sb", anc)
+
+        half = S // 2
+        w_dealt = sb.tile([P, PACK, P, PACK], BF16, name="w_dealt", align_bytes=64)
+
+        def deal_w(engine_copy, m0, m1, walk):
+            engine_copy(
+                w_dealt[:, :, m0:m1, :].rearrange("p t m j -> " + walk),
+                w_raw[:, :, PACK * m0 : PACK * m1].rearrange("p j (m t) -> " + walk, t=PACK),
+            )
+
+        deal_w(nc.scalar.copy, 0, 64, "p m t j")
+        deal_w(nc.vector.tensor_copy, 64, 128, "p m j t")
+        xq_scales = gathered("xq_scales", x_scale_table, offs_sb, U8)
+
+        w_words = sb.tile([P, H], U32, name="w_words", align_bytes=64)
+        w_scales = sb.tile([P, H], U8, name="w_scales", align_bytes=64)
+        nc.vector.quantize_mx(
+            out=w_words[:].bitcast(FP8X4), scales=w_scales[:], in_=w_dealt[:].rearrange("p t m j -> p (t m j)")
+        )
+        xq_words = sb.tile([P, S], U32, name="xq_words", align_bytes=64)
+        for c in range(0, S, half):
+            nc.vector.tensor_copy(xq_words[:, c : c + half], x_word_table[:].indirect(entries(offs_sb, c, half)))
+
+        def first_product(name, t, c0, c1):
+            rows = slice(t * P, (t + 1) * P)
+            bank = psum.tile([P, c1 - c0], F32, name=name)
+            nc.tensor.matmul_mx(
+                out=bank[:],
+                lhsT=w_words[:, rows].bitcast(FP8X4),
+                lhsT_scale=w_scales[:, rows],
+                rhs=xq_words[:, c0:c1].bitcast(FP8X4),
+                rhs_scale=xq_scales[:, c0:c1],
+                start=True,
+                stop=True,
+            )
+            return bank
+
+        def window(name, width):
+            tile = sb.tile([P, width + PER_COL], F32, name=name)
+            nc.gpsimd.memset(tile[:, width:], 0.0)
+            return tile
+
+        y_sbs = [window(f"y_sb{t}", S) for t in range(PACK)]
+        for c in range(0, S, half):
+            bank = first_product(f"y_ps0_{c}", 0, c, c + half)
+            nc.scalar.copy(y_sbs[0][:, c : c + half], bank[:])
+        y_ps = [y_sbs[0][:, :S]] + [first_product(f"y_ps{t}", t, 0, S)[:] for t in range(1, PACK)]
+        eq_scales = gathered("eq_scales", e_scale_table, prt_sb, U8)
+
+        def scalar_gather(dst, table, offsets):
+            nc.scalar.activation(dst, table[:].indirect(offsets), ACT.Copy)
+
+        def vector_gather(dst, table, offsets):
+            nc.vector.tensor_copy(dst, table[:].indirect(offsets))
+
+        def plane_tiles(name):
+            return [sb.tile([P, S], F32, name=f"{name}{t}") for t in range(PACK)]
+
+        y1, y2 = (plane_tiles(n) for n in ("y1_", "y2_"))
+        low = [sb.tile([P, S], F32, name=f"low{t}") for t in range(2)]
+        high = [sb.tile([P, S], F32, name=f"high{t}") for t in range(2)]
+        last = PACK - 1
+        rng = [sb.tile([P, S], F32, name=f"rng{t}") for t in range(last)]
+        picked = sb.tile([P, PACK, V], F32, name="picked")
+        picked_low = sb.tile([P, V], F32, name="picked_low")
+        hid_low = sb.tile([P, V], F32, name="hid_low")
+        eq_words = gathered("eq_words", e_word_table, prt_sb, U32)
+        late = sb.tile([P, 4 * S + PACK * V], F32, name="e_word_table")
+        low.extend([late[:, 0:S], late[:, S : 2 * S]])
+        high.extend([late[:, 2 * S : 3 * S], late[:, 3 * S : 4 * S]])
+        hid = late[:, 4 * S :].rearrange("p (t v) -> p t v", t=PACK)
+        exq_unit = sb.tile([P, PACK, V], F32, name="exq_unit")
+        for t in range(PACK):
+            nc.gpsimd.tensor_scalar(exq_unit[:, t, :], exq_sb[:, t, :], unit_sb[:, t : t + 1], 0.0, ALU.mult, ALU.add)
+
+        def scale_and_join(dst, src, t, other, op):
+            nc.vector.scalar_tensor_tensor(dst, src, unit_sb[:, t : t + 1], other, ALU.mult, op)
+
+        def finish_plane(t):
+            scale_and_join(hid[:, t, :], picked[:, t, :], t, exq_unit[:, t, :], ALU.subtract)
+
+        for t in range(last):
+            scalar_gather(y1[t][:], y_sbs[t], bm1_sb[:])
+            nc.scalar.copy(y_sbs[t + 1][:, :S], y_ps[t + 1])
+            on_scalar = t * half
+            if on_scalar:
+                scalar_gather(y2[t][:, :on_scalar], y_sbs[t], entries(bm2_sb, 0, on_scalar))
+            for c in range(on_scalar, S, half):
+                vector_gather(y2[t][:, c : c + half], y_sbs[t], entries(bm2_sb, c, half))
+            if t == 2:
+                finish_plane(0)
+            nc.vector.tensor_tensor(low[t][:], y1[t][:], y_ps[t], ALU.min)
+            if t == 1:
+                vector_gather(picked[:, 0, :], rng[0], ps_sb[:])
+            nc.vector.tensor_tensor(high[t][:], y2[t][:], y_ps[t], ALU.max)
+            nc.vector.tensor_tensor(rng[t][:], low[t][:], high[t][:], ALU.add)
+
+        scalar_gather(y1[last][:], y_sbs[last], bm1_sb[:])
+        nc.vector.tensor_tensor(low[last][:], y1[last][:], y_ps[last], ALU.min)
+        for c in range(0, S, half):
+            cols = slice(c, c + half)
+            scalar_gather(y2[last][:, cols], y_sbs[last], entries(bm2_sb, c, half))
+            nc.vector.tensor_tensor(high[last][:, cols], y2[last][:, cols], y_ps[last][:, cols], ALU.max)
+        for t in range(1, last):
+            scalar_gather(picked[:, t, :], rng[t], ps_sb[:])
+        finish_plane(1)
+        scalar_gather(picked_low[:], low[last], ps_sb[:])
+        vector_gather(picked[:, last, :P], high[last], entries(ps_sb, 0, P))
+        scalar_gather(picked[:, last, P:], high[last], entries(ps_sb, P, P))
+        finish_plane(last - 1)
+        scale_and_join(hid_low[:], picked_low[:], last, exq_unit[:, last, :], ALU.subtract)
+
+        dealt = []
+        for a in range(2):
+            poses = slice(a * P, (a + 1) * P)
+            scale_and_join(hid[:, last, poses], picked[:, last, poses], last, hid_low[:, poses], ALU.add)
+        for a in range(2):
+            poses = slice(a * P, (a + 1) * P)
+            tile = sb.tile([P, P, PACK], BF16, name=f"hid_dealt{a}", align_bytes=64)
+            nc.vector.tensor_copy(
+                tile[:].rearrange("p (c i) t -> p c t i", i=4), hid[:, :, poses].rearrange("p t (c i) -> p c t i", i=4)
+            )
+            dealt.append(tile)
+        wgt_picked = sb.tile([P, Z], F32, name=f"y2_{last}")
+        scalar_gather(wgt_picked[:], wgt_sb, prt_sb[:])
+        sc_ps = []
+        for a in range(2):
+            h_words = sb.tile([P, P], U32, name=f"h_words{a}", align_bytes=64)
+            h_scales = sb.tile([P, P], U8, name=f"h_scales{a}", align_bytes=64)
+            nc.vector.quantize_mx(
+                out=h_words[:].bitcast(FP8X4), scales=h_scales[:], in_=dealt[a][:].rearrange("p v t -> p (v t)")
+            )
+            banks = []
+            for c in range(0, Z, half):
+                bank = psum.tile([P, half], F32, name=f"y_ps0_{c}" if a == 0 else f"sc_ps{c}")
+                nc.tensor.matmul_mx(
+                    out=bank[:],
+                    lhsT=h_words[:].bitcast(FP8X4),
+                    lhsT_scale=h_scales[:],
+                    rhs=eq_words[:, c : c + half].bitcast(FP8X4),
+                    rhs_scale=eq_scales[:, c : c + half],
+                    start=True,
+                    stop=True,
+                )
+                banks.append(bank)
+            sc_ps.append(banks)
+
+        def row_tiles(name, width):
+            return [sb.tile([P, width], F32, name=f"{name}{a}") for a in range(2)]
+
+        tanh_sc, tanh_sq, like = (row_tiles(n, Z) for n in ("tanh_sc", "tanh_sq", "like"))
+        pw = [window(f"pw{a}", Z) for a in range(2)]
+        nw, pw_anc, res = (row_tiles(n, Z) for n in ("nw", "pw_anc", "res"))
+        pw_sum = sb.tile([P, 2], F32, name="pw_sum")
+        denom = sb.tile([P, 2], F32, name="denom")
+        half_inv = sb.tile([P, 2], F32, name="half_inv")
+        for a in range(2):
+            for n, c in enumerate(range(0, Z, half)):
+                cols = slice(c, c + half)
+                nc.scalar.activation(tanh_sc[a][:, cols], sc_ps[a][n][:], ACT.Tanh)
+                nc.vector.tensor_tensor(tanh_sq[a][:, cols], tanh_sc[a][:, cols], tanh_sc[a][:, cols], ALU.mult)
+        for a in range(2):
+            nc.scalar.activation(like[a][:], tanh_sq[a][:], ACT.Exp, scale=-2.0)
+            nc.vector.scalar_tensor_tensor(
+                pw[a][:, :Z], like[a][:], 1.0, wgt_picked[:], ALU.mult, ALU.mult, accum_out=pw_sum[:, a : a + 1]
+            )
+        tail = Z - P
+        nc.vector.tensor_scalar(denom[:], pw_sum[:], 2.0 / Z, 0.2, ALU.mult, ALU.add)
+        vector_gather(pw_anc[1][:, tail:], pw[1], entries(anc_sb, tail, P))
+        nc.vector.reciprocal(half_inv[:], denom[:])
+        for a in range(2):
+            nc.vector.tensor_scalar(nw[a][:], pw[a][:, :Z], half_inv[:, a : a + 1], 2.0, ALU.mult, ALU.mult)
+
+        def finish(a, cols):
+            nc.vector.scalar_tensor_tensor(
+                res[a][:, cols], pw_anc[a][:, cols], half_inv[:, a : a + 1], nw[a][:, cols], ALU.mult, ALU.add
+            )
+            nc.sync.dma_start(out[a * P : (a + 1) * P, cols], res[a][:, cols])
+
+        scalar_gather(pw_anc[0][:], pw[0], anc_sb[:])
+        finish(0, slice(0, Z))
+        scalar_gather(pw_anc[1][:, :tail], pw[1], entries(anc_sb, 0, tail))
+        finish(1, slice(0, Z))

@@ -115,10 +115,20 @@ def tile_picked_ymaprel_res_p_kernel(
             return tile
 
         y_sbs = [window(f"y_sb{t}", S) for t in range(PACK)]
+        first_banks = []
         for c in range(0, S, half):
             bank = first_product(f"y_ps0_{c}", 0, c, c + half)
             nc.scalar.copy(y_sbs[0][:, c : c + half], bank[:])
-        y_ps = [y_sbs[0][:, :S]] + [first_product(f"y_ps{t}", t, 0, S)[:] for t in range(1, PACK)]
+            first_banks.append(bank)
+        y_ps = [None] + [first_product(f"y_ps{t}", t, 0, S)[:] for t in range(1, PACK)]
+
+        def with_y(dst, picked_y, t, op):
+            if t > 0:
+                nc.vector.tensor_tensor(dst[:], picked_y[:], y_ps[t], op)
+            else:
+                for n, c in enumerate(range(0, S, half)):
+                    nc.vector.tensor_tensor(dst[:, c : c + half], picked_y[:, c : c + half], first_banks[n][:], op)
+
         eq_scales = gathered("eq_scales", e_scale_table, prt_sb, U8)
 
         def scalar_gather(dst, table, offsets):
@@ -156,18 +166,19 @@ def tile_picked_ymaprel_res_p_kernel(
         for t in range(last):
             scalar_gather(y1[t][:], y_sbs[t], bm1_sb[:])
             nc.scalar.copy(y_sbs[t + 1][:, :S], y_ps[t + 1])
-            on_scalar = t * half
-            if on_scalar:
-                scalar_gather(y2[t][:, :on_scalar], y_sbs[t], entries(bm2_sb, 0, on_scalar))
-            for c in range(on_scalar, S, half):
-                vector_gather(y2[t][:, c : c + half], y_sbs[t], entries(bm2_sb, c, half))
+            if t == 2:
+                scalar_gather(y2[t][:], y_sbs[t], bm2_sb[:])
+            else:
+                for c in range(0, S, half):
+                    vector_gather(y2[t][:, c : c + half], y_sbs[t], entries(bm2_sb, c, half))
             if t == 2:
                 finish_plane(0)
-            nc.vector.tensor_tensor(low[t][:], y1[t][:], y_ps[t], ALU.min)
+            with_y(low[t], y1[t], t, ALU.min)
             if t == 1:
                 vector_gather(picked[:, 0, :], rng[0], ps_sb[:])
-            nc.vector.tensor_tensor(high[t][:], y2[t][:], y_ps[t], ALU.max)
-            nc.vector.tensor_tensor(rng[t][:], low[t][:], high[t][:], ALU.add)
+            with_y(high[t], y2[t], t, ALU.max)
+            adder = nc.gpsimd if t < 2 else nc.vector
+            adder.tensor_tensor(rng[t][:], low[t][:], high[t][:], ALU.add)
 
         scalar_gather(y1[last][:], y_sbs[last], bm1_sb[:])
         nc.vector.tensor_tensor(low[last][:], y1[last][:], y_ps[last], ALU.min)
@@ -179,24 +190,23 @@ def tile_picked_ymaprel_res_p_kernel(
             scalar_gather(picked[:, t, :], rng[t], ps_sb[:])
         finish_plane(1)
         scalar_gather(picked_low[:], low[last], ps_sb[:])
-        vector_gather(picked[:, last, :P], high[last], entries(ps_sb, 0, P))
+        scalar_gather(picked[:, last, :P], high[last], entries(ps_sb, 0, P))
         scalar_gather(picked[:, last, P:], high[last], entries(ps_sb, P, P))
         finish_plane(last - 1)
         scale_and_join(hid_low[:], picked_low[:], last, exq_unit[:, last, :], ALU.subtract)
 
         dealt = []
-        for a in range(2):
+        for a, engine_copy in enumerate((nc.vector.tensor_copy, nc.scalar.copy)):
             poses = slice(a * P, (a + 1) * P)
             scale_and_join(hid[:, last, poses], picked[:, last, poses], last, hid_low[:, poses], ALU.add)
-        for a in range(2):
-            poses = slice(a * P, (a + 1) * P)
             tile = sb.tile([P, P, PACK], BF16, name=f"hid_dealt{a}", align_bytes=64)
-            nc.vector.tensor_copy(
+            engine_copy(
                 tile[:].rearrange("p (c i) t -> p c t i", i=4), hid[:, :, poses].rearrange("p t (c i) -> p c t i", i=4)
             )
             dealt.append(tile)
-        wgt_picked = sb.tile([P, Z], F32, name=f"y2_{last}")
-        scalar_gather(wgt_picked[:], wgt_sb, prt_sb[:])
+        wgt_picked = sb.tile([P, Z + PER_COL], F32, name=f"y2_{last}")
+        nc.gpsimd.memset(wgt_picked[:, Z:], 1.0)
+        scalar_gather(wgt_picked[:, :Z], wgt_sb, prt_sb[:])
         sc_ps = []
         for a in range(2):
             h_words = sb.tile([P, P], U32, name=f"h_words{a}", align_bytes=64)
@@ -222,36 +232,34 @@ def tile_picked_ymaprel_res_p_kernel(
         def row_tiles(name, width):
             return [sb.tile([P, width], F32, name=f"{name}{a}") for a in range(2)]
 
-        tanh_sc, tanh_sq, like = (row_tiles(n, Z) for n in ("tanh_sc", "tanh_sq", "like"))
-        pw = [window(f"pw{a}", Z) for a in range(2)]
+        tanh_sc, tanh_sq = (row_tiles(n, Z) for n in ("tanh_sc", "tanh_sq"))
+        like, pw = (row_tiles(n, Z + PER_COL) for n in ("like", "pw"))
         nw, pw_anc, res = (row_tiles(n, Z) for n in ("nw", "pw_anc", "res"))
-        pw_sum = sb.tile([P, 2], F32, name="pw_sum")
-        denom = sb.tile([P, 2], F32, name="denom")
-        half_inv = sb.tile([P, 2], F32, name="half_inv")
+        pw_sum, inv = (row_tiles(n, 1) for n in ("pw_sum", "inv"))
+        ones = sb.tile([P, PER_COL], F32, name="ones")
+        nc.gpsimd.memset(ones[:], 1.0)
+        for a in range(2):
+            nc.gpsimd.tensor_scalar(like[a][:, Z:], ones[:], 0.1 * Z / PER_COL, 0.0, ALU.mult, ALU.add)
         for a in range(2):
             for n, c in enumerate(range(0, Z, half)):
                 cols = slice(c, c + half)
                 nc.scalar.activation(tanh_sc[a][:, cols], sc_ps[a][n][:], ACT.Tanh)
                 nc.vector.tensor_tensor(tanh_sq[a][:, cols], tanh_sc[a][:, cols], tanh_sc[a][:, cols], ALU.mult)
         for a in range(2):
-            nc.scalar.activation(like[a][:], tanh_sq[a][:], ACT.Exp, scale=-2.0)
+            nc.scalar.activation(like[a][:, :Z], tanh_sq[a][:], ACT.Exp, scale=-2.0)
             nc.vector.scalar_tensor_tensor(
-                pw[a][:, :Z], like[a][:], 1.0, wgt_picked[:], ALU.mult, ALU.mult, accum_out=pw_sum[:, a : a + 1]
+                pw[a][:], like[a][:], 1.0, wgt_picked[:], ALU.mult, ALU.mult, accum_out=pw_sum[a][:]
             )
-        tail = Z - P
-        nc.vector.tensor_scalar(denom[:], pw_sum[:], 2.0 / Z, 0.2, ALU.mult, ALU.add)
-        vector_gather(pw_anc[1][:, tail:], pw[1], entries(anc_sb, tail, P))
-        nc.vector.reciprocal(half_inv[:], denom[:])
         for a in range(2):
-            nc.vector.tensor_scalar(nw[a][:], pw[a][:, :Z], half_inv[:, a : a + 1], 2.0, ALU.mult, ALU.mult)
-
-        def finish(a, cols):
-            nc.vector.scalar_tensor_tensor(
-                res[a][:, cols], pw_anc[a][:, cols], half_inv[:, a : a + 1], nw[a][:, cols], ALU.mult, ALU.add
-            )
-            nc.sync.dma_start(out[a * P : (a + 1) * P, cols], res[a][:, cols])
-
-        scalar_gather(pw_anc[0][:], pw[0], anc_sb[:])
-        finish(0, slice(0, Z))
-        scalar_gather(pw_anc[1][:, :tail], pw[1], entries(anc_sb, 0, tail))
-        finish(1, slice(0, Z))
+            nc.vector.reciprocal(inv[a][:], pw_sum[a][:])
+        for a in range(2):
+            nc.vector.tensor_scalar(nw[a][:], pw[a][:, :Z], inv[a][:], float(Z), ALU.mult, ALU.mult)
+        for a in range(2):
+            step = Z if a == 0 else half
+            for c in range(0, Z, step):
+                cols = slice(c, c + step)
+                nc.scalar.activation(pw_anc[a][:, cols], pw[a][:].indirect(entries(anc_sb, c, step)), ACT.Copy, scale=0.5 * Z)
+                nc.vector.scalar_tensor_tensor(
+                    res[a][:, cols], pw_anc[a][:, cols], inv[a][:], nw[a][:, cols], ALU.mult, ALU.add
+                )
+                nc.sync.dma_start(out[a * P : (a + 1) * P, cols], res[a][:, cols])

@@ -83,7 +83,7 @@ def tile_picked_ymaprel_res_p_kernel(
             )
 
         deal_w(nc.scalar.copy, 0, 64, "p m t j")
-        deal_w(nc.vector.tensor_copy, 64, 128, "p m j t")
+        deal_w(nc.vector.tensor_copy, 64, 128, "p m t j")
         xq_scales = gathered("xq_scales", x_scale_table, offs_sb, U8)
 
         w_words = sb.tile([P, H], U32, name="w_words", align_bytes=64)
@@ -153,15 +153,18 @@ def tile_picked_ymaprel_res_p_kernel(
         low.extend([late[:, 0:S], late[:, S : 2 * S]])
         high.extend([late[:, 2 * S : 3 * S], late[:, 3 * S : 4 * S]])
         hid = late[:, 4 * S :].rearrange("p (t v) -> p t v", t=PACK)
-        exq_unit = sb.tile([P, PACK, V], F32, name="exq_unit")
-        for t in range(PACK):
-            nc.gpsimd.tensor_scalar(exq_unit[:, t, :], exq_sb[:, t, :], unit_sb[:, t : t + 1], 0.0, ALU.mult, ALU.add)
+        exq_unit = []
+
+        def scale_exq(t):
+            tile = sb.tile([P, V], F32, name=f"y1_{t}")
+            nc.gpsimd.tensor_scalar(tile[:], exq_sb[:, t, :], unit_sb[:, t : t + 1], 0.0, ALU.mult, ALU.add)
+            exq_unit.append(tile)
 
         def scale_and_join(dst, src, t, other, op):
             nc.vector.scalar_tensor_tensor(dst, src, unit_sb[:, t : t + 1], other, ALU.mult, op)
 
         def finish_plane(t):
-            scale_and_join(hid[:, t, :], picked[:, t, :], t, exq_unit[:, t, :], ALU.subtract)
+            scale_and_join(hid[:, t, :], picked[:, t, :], t, exq_unit[t][:], ALU.subtract)
 
         for t in range(last):
             scalar_gather(y1[t][:], y_sbs[t], bm1_sb[:])
@@ -171,29 +174,27 @@ def tile_picked_ymaprel_res_p_kernel(
             else:
                 for c in range(0, S, half):
                     vector_gather(y2[t][:, c : c + half], y_sbs[t], entries(bm2_sb, c, half))
-            if t == 2:
-                finish_plane(0)
             with_y(low[t], y1[t], t, ALU.min)
-            if t == 1:
-                vector_gather(picked[:, 0, :], rng[0], ps_sb[:])
+            scale_exq(t)
             with_y(high[t], y2[t], t, ALU.max)
-            adder = nc.gpsimd if t < 2 else nc.vector
-            adder.tensor_tensor(rng[t][:], low[t][:], high[t][:], ALU.add)
+            nc.vector.tensor_tensor(rng[t][:], low[t][:], high[t][:], ALU.add)
 
         scalar_gather(y1[last][:], y_sbs[last], bm1_sb[:])
         nc.vector.tensor_tensor(low[last][:], y1[last][:], y_ps[last], ALU.min)
+        scale_exq(last)
         for c in range(0, S, half):
             cols = slice(c, c + half)
             scalar_gather(y2[last][:, cols], y_sbs[last], entries(bm2_sb, c, half))
             nc.vector.tensor_tensor(high[last][:, cols], y2[last][:, cols], y_ps[last][:, cols], ALU.max)
-        for t in range(1, last):
+        for t in range(last):
             scalar_gather(picked[:, t, :], rng[t], ps_sb[:])
+        finish_plane(0)
         finish_plane(1)
         scalar_gather(picked_low[:], low[last], ps_sb[:])
         scalar_gather(picked[:, last, :P], high[last], entries(ps_sb, 0, P))
         scalar_gather(picked[:, last, P:], high[last], entries(ps_sb, P, P))
         finish_plane(last - 1)
-        scale_and_join(hid_low[:], picked_low[:], last, exq_unit[:, last, :], ALU.subtract)
+        scale_and_join(hid_low[:], picked_low[:], last, exq_unit[last][:], ALU.subtract)
 
         dealt = []
         for a, engine_copy in enumerate((nc.vector.tensor_copy, nc.scalar.copy)):

from contextlib import ExitStack

import concourse.mybir as mybir

K, T, S, H, V, Z, W = 512, 2048, 512, 512, 256, 512, 2048
FLOPS = 2 * K * H * S + 2 * H * V * Z

F32 = mybir.dt.float32
BF16 = mybir.dt.bfloat16
I32 = mybir.dt.int32
U32 = mybir.dt.uint32
U16 = mybir.dt.uint16
U8 = mybir.dt.uint8
FP8X4 = mybir.dt.float8_e4m3fn_x4
ALU = mybir.AluOpType
ACT = mybir.ActivationFunctionType

P = 128
PACK = 4
PER_COL = 16


def entries(offsets, first, count):
    return offsets[:, first // PER_COL : (first + count) // PER_COL]


def tile_picked_ymaprel_res_p_kernel(
    tc, x_words, x_scales, w1, e_words, e_scales, exq, unit, wgt, offs, bm1, bm2, ps, prt, anc, out
):
    nc = tc.nc
    with ExitStack() as ctx:
        sb = ctx.enter_context(tc.tile_pool(name="sb", bufs=1))
        psum = ctx.enter_context(tc.psum_pool(name="psum", bufs=1))

        def load_list(name, src):
            tile = sb.tile(list(src.shape), U16, name=name)
            nc.sync.dma_start(tile[:], src)
            return tile

        def load_words(name, src):
            tile = sb.tile([P, src.shape[2]], U32, name=name)
            nc.sync.dma_start(tile[:].bitcast(I32), src[0].rearrange("p n t -> p (n t)").bitcast(I32))
            return tile

        def load_scales(name, src, queue):
            tile = sb.tile([P, src.shape[2]], U8, name=name)
            nc.vector.memset(tile[:].bitcast(I32), 0)
            for q in range(4):
                queue.dma_start(tile[32 * q : 32 * q + 4, :].bitcast(I32), src[0, 4 * q : 4 * q + 4, :].bitcast(I32))
            return tile

        def gathered(name, table, offsets, dtype):
            tile = sb.tile([P, offsets.shape[1] * PER_COL], dtype, name=name, align_bytes=64)
            nc.vector.tensor_copy(tile[:], table[:].indirect(offsets[:]))
            return tile

        offs_sb = load_list("offs_sb", offs)
        w_raw = sb.tile([P, PACK, H], F32, name="w_raw")
        nc.sync.dma_start(w_raw[:], w1.rearrange("(p j) c -> p j c", j=PACK))
        x_scale_table = load_scales("x_scale_table", x_scales, nc.sync)
        x_word_table = load_words("x_word_table", x_words)
        bm1_sb = load_list("bm1_sb", bm1)
        bm2_sb = load_list("bm2_sb", bm2)
        prt_sb = load_list("prt_sb", prt)
        e_scale_table = load_scales("e_scale_table", e_scales, nc.sync)
        exq_sb = sb.tile([P, PACK, V], F32, name="exq_sb")
        nc.sync.dma_start(exq_sb[:], exq.rearrange("(p t) v -> p t v", t=PACK))
        ps_sb = load_list("ps_sb", ps)
        unit_sb = sb.tile([P, PACK], F32, name="unit_sb")
        nc.sync.dma_start(unit_sb[:], unit.rearrange("(p t) o -> p (t o)", t=PACK))
        wgt_sb = sb.tile([P, W], F32, name="wgt_sb")
        nc.sync.dma_start(wgt_sb[:], wgt)
        e_word_table = load_words("e_word_table", e_words)
        anc_sb = load_list("anc_sb", anc)

        half = S // 2
        w_dealt = sb.tile([P, PACK, P, PACK], BF16, name="w_dealt", align_bytes=64)

        def deal_w(engine_copy, m0, m1, walk):
            engine_copy(
                w_dealt[:, :, m0:m1, :].rearrange("p t m j -> " + walk),
                w_raw[:, :, PACK * m0 : PACK * m1].rearrange("p j (m t) -> " + walk, t=PACK),
            )

        deal_w(nc.scalar.copy, 0, 64, "p m t j")
        deal_w(nc.vector.tensor_copy, 64, 128, "p m t j")
        xq_scales = gathered("xq_scales", x_scale_table, offs_sb, U8)

        w_words = sb.tile([P, H], U32, name="w_words", align_bytes=64)
        w_scales = sb.tile([P, H], U8, name="w_scales", align_bytes=64)
        nc.vector.quantize_mx(
            out=w_words[:].bitcast(FP8X4), scales=w_scales[:], in_=w_dealt[:].rearrange("p t m j -> p (t m j)")
        )
        xq_words = sb.tile([P, S], U32, name="xq_words", align_bytes=64)
        for c in range(0, S, half):
            nc.vector.tensor_copy(xq_words[:, c : c + half], x_word_table[:].indirect(entries(offs_sb, c, half)))

        def first_product(name, t, c0, c1):
            rows = slice(t * P, (t + 1) * P)
            bank = psum.tile([P, c1 - c0], F32, name=name)
            nc.tensor.matmul_mx(
                out=bank[:],
                lhsT=w_words[:, rows].bitcast(FP8X4),
                lhsT_scale=w_scales[:, rows],
                rhs=xq_words[:, c0:c1].bitcast(FP8X4),
                rhs_scale=xq_scales[:, c0:c1],
                start=True,
                stop=True,
            )
            return bank

        def window(name, width):
            tile = sb.tile([P, width + PER_COL], F32, name=name)
            nc.gpsimd.memset(tile[:, width:], 0.0)
            return tile

        y_sbs = [window(f"y_sb{t}", S) for t in range(PACK)]
        first_banks = []
        for c in range(0, S, half):
            bank = first_product(f"y_ps0_{c}", 0, c, c + half)
            nc.scalar.copy(y_sbs[0][:, c : c + half], bank[:])
            first_banks.append(bank)
        y_ps = [None] + [first_product(f"y_ps{t}", t, 0, S)[:] for t in range(1, PACK)]

        def with_y(dst, picked_y, t, op):
            if t > 0:
                nc.vector.tensor_tensor(dst[:], picked_y[:], y_ps[t], op)
            else:
                for n, c in enumerate(range(0, S, half)):
                    nc.vector.tensor_tensor(dst[:, c : c + half], picked_y[:, c : c + half], first_banks[n][:], op)

        eq_scales = gathered("eq_scales", e_scale_table, prt_sb, U8)

        def scalar_gather(dst, table, offsets):
            nc.scalar.activation(dst, table[:].indirect(offsets), ACT.Copy)

        def vector_gather(dst, table, offsets):
            nc.vector.tensor_copy(dst, table[:].indirect(offsets))

        def plane_tiles(name):
            return [sb.tile([P, S], F32, name=f"{name}{t}") for t in range(PACK)]

        y1, y2 = (plane_tiles(n) for n in ("y1_", "y2_"))
        low = [sb.tile([P, S], F32, name=f"low{t}") for t in range(2)]
        high = [sb.tile([P, S], F32, name=f"high{t}") for t in range(2)]
        last = PACK - 1
        rng = [sb.tile([P, S], F32, name=f"rng{t}") for t in range(last)]
        picked = sb.tile([P, PACK, V], F32, name="picked")
        picked_low = sb.tile([P, V], F32, name="picked_low")
        hid_low = sb.tile([P, V], F32, name="hid_low")
        eq_words = gathered("eq_words", e_word_table, prt_sb, U32)
        late = sb.tile([P, 4 * S + PACK * V], F32, name="e_word_table")
        low.extend([late[:, 0:S], late[:, S : 2 * S]])
        high.extend([late[:, 2 * S : 3 * S], late[:, 3 * S : 4 * S]])
        hid = late[:, 4 * S :].rearrange("p (t v) -> p t v", t=PACK)
        exq_unit = []

        def scale_exq(t):
            tile = sb.tile([P, V], F32, name=f"y1_{t}")
            nc.gpsimd.tensor_scalar(tile[:], exq_sb[:, t, :], unit_sb[:, t : t + 1], 0.0, ALU.mult, ALU.add)
            exq_unit.append(tile)

        def scale_and_join(dst, src, t, other, op):
            nc.vector.scalar_tensor_tensor(dst, src, unit_sb[:, t : t + 1], other, ALU.mult, op)

        def finish_plane(t):
            scale_and_join(hid[:, t, :], picked[:, t, :], t, exq_unit[t][:], ALU.subtract)

        for t in range(last):
            scalar_gather(y1[t][:], y_sbs[t], bm1_sb[:])
            nc.scalar.copy(y_sbs[t + 1][:, :S], y_ps[t + 1])
            if t == 2:
                scalar_gather(y2[t][:], y_sbs[t], bm2_sb[:])
            else:
                for c in range(0, S, half):
                    vector_gather(y2[t][:, c : c + half], y_sbs[t], entries(bm2_sb, c, half))
            with_y(low[t], y1[t], t, ALU.min)
            scale_exq(t)
            with_y(high[t], y2[t], t, ALU.max)
            nc.vector.tensor_tensor(rng[t][:], low[t][:], high[t][:], ALU.add)

        scalar_gather(y1[last][:], y_sbs[last], bm1_sb[:])
        nc.vector.tensor_tensor(low[last][:], y1[last][:], y_ps[last], ALU.min)
        scale_exq(last)
        for c in range(0, S, half):
            cols = slice(c, c + half)
            scalar_gather(y2[last][:, cols], y_sbs[last], entries(bm2_sb, c, half))
            nc.vector.tensor_tensor(high[last][:, cols], y2[last][:, cols], y_ps[last][:, cols], ALU.max)
        for t in range(last):
            scalar_gather(picked[:, t, :], rng[t], ps_sb[:])
        finish_plane(0)
        finish_plane(1)
        scalar_gather(picked_low[:], low[last], ps_sb[:])
        scalar_gather(picked[:, last, :P], high[last], entries(ps_sb, 0, P))
        scalar_gather(picked[:, last, P:], high[last], entries(ps_sb, P, P))
        finish_plane(last - 1)
        scale_and_join(hid_low[:], picked_low[:], last, exq_unit[last][:], ALU.subtract)

        dealt = []
        for a, engine_copy in enumerate((nc.vector.tensor_copy, nc.scalar.copy)):
            poses = slice(a * P, (a + 1) * P)
            scale_and_join(hid[:, last, poses], picked[:, last, poses], last, hid_low[:, poses], ALU.add)
            tile = sb.tile([P, P, PACK], BF16, name=f"hid_dealt{a}", align_bytes=64)
            engine_copy(
                tile[:].rearrange("p (c i) t -> p c t i", i=4), hid[:, :, poses].rearrange("p t (c i) -> p c t i", i=4)
            )
            dealt.append(tile)
        wgt_picked = sb.tile([P, Z + PER_COL], F32, name=f"y2_{last}")
        nc.gpsimd.memset(wgt_picked[:, Z:], 1.0)
        scalar_gather(wgt_picked[:, :Z], wgt_sb, prt_sb[:])
        sc_ps = []
        for a in range(2):
            h_words = sb.tile([P, P], U32, name=f"h_words{a}", align_bytes=64)
            h_scales = sb.tile([P, P], U8, name=f"h_scales{a}", align_bytes=64)
            nc.vector.quantize_mx(
                out=h_words[:].bitcast(FP8X4), scales=h_scales[:], in_=dealt[a][:].rearrange("p v t -> p (v t)")
            )
            banks = []
            for c in range(0, Z, half):
                bank = psum.tile([P, half], F32, name=f"y_ps0_{c}" if a == 0 else f"sc_ps{c}")
                nc.tensor.matmul_mx(
                    out=bank[:],
                    lhsT=h_words[:].bitcast(FP8X4),
                    lhsT_scale=h_scales[:],
                    rhs=eq_words[:, c : c + half].bitcast(FP8X4),
                    rhs_scale=eq_scales[:, c : c + half],
                    start=True,
                    stop=True,
                )
                banks.append(bank)
            sc_ps.append(banks)

        def row_tiles(name, width):
            return [sb.tile([P, width], F32, name=f"{name}{a}") for a in range(2)]

        tanh_sc, tanh_sq = (row_tiles(n, Z) for n in ("tanh_sc", "tanh_sq"))
        like, pw = (row_tiles(n, Z + PER_COL) for n in ("like", "pw"))
        nw, pw_anc, res = (row_tiles(n, Z) for n in ("nw", "pw_anc", "res"))
        pw_sum, inv = (row_tiles(n, 1) for n in ("pw_sum", "inv"))
        ones = sb.tile([P, PER_COL], F32, name="ones")
        nc.gpsimd.memset(ones[:], 1.0)
        for a in range(2):
            nc.gpsimd.tensor_scalar(like[a][:, Z:], ones[:], 0.1 * Z / PER_COL, 0.0, ALU.mult, ALU.add)
        for a in range(2):
            for n, c in enumerate(range(0, Z, half)):
                cols = slice(c, c + half)
                nc.scalar.activation(tanh_sc[a][:, cols], sc_ps[a][n][:], ACT.Tanh)
                nc.vector.tensor_tensor(tanh_sq[a][:, cols], tanh_sc[a][:, cols], tanh_sc[a][:, cols], ALU.mult)
        for a in range(2):
            nc.scalar.activation(like[a][:, :Z], tanh_sq[a][:], ACT.Exp, scale=-2.0)
            nc.vector.scalar_tensor_tensor(
                pw[a][:], like[a][:], 1.0, wgt_picked[:], ALU.mult, ALU.mult, accum_out=pw_sum[a][:]
            )
        for a in range(2):
            nc.vector.reciprocal(inv[a][:], pw_sum[a][:])
        for a in range(2):
            nc.vector.tensor_scalar(nw[a][:], pw[a][:, :Z], inv[a][:], float(Z), ALU.mult, ALU.mult)
        for a in range(2):
            step = Z if a == 0 else half
            for c in range(0, Z, step):
                cols = slice(c, c + step)
                nc.scalar.activation(pw_anc[a][:, cols], pw[a][:].indirect(entries(anc_sb, c, step)), ACT.Copy, scale=0.5 * Z)
                nc.vector.scalar_tensor_tensor(
                    res[a][:, cols], pw_anc[a][:, cols], inv[a][:], nw[a][:, cols], ALU.mult, ALU.add
                )
                nc.sync.dma_start(out[a * P : (a + 1) * P, cols], res[a][:, cols])
